import numpy as np
import ml_dtypes


def mxq(x, axis, fmt="e4m3"):
    dtype, down = {"e4m3": (ml_dtypes.float8_e4m3fn, 7), "e5m2": (ml_dtypes.float8_e5m2, 14)}[fmt]
    v = np.moveaxis(np.asarray(x, np.float32).astype(ml_dtypes.bfloat16).astype(np.float64), axis, -1)
    blocks = v.reshape(v.shape[:-1] + (-1, 32))
    amax = np.abs(blocks).max(-1, keepdims=True)
    byte = np.maximum(np.where(amax > 0, np.frexp(amax)[1] - 1 + 127, 0) - down, 1)
    scale = np.exp2(byte - 127.0)
    codes = (blocks / scale).astype(np.float32).astype(dtype).astype(np.float64)
    return np.moveaxis((codes * scale).reshape(v.shape), -1, axis)


WIDE = False


def mx_kscale(k):
    if not WIDE:
        return np.ones(k)
    levels = np.array([10, -10, 5, -5, 0])
    if k % 512:
        return np.exp2(np.random.permutation(np.resize(levels, k // 32))).repeat(32)
    a = np.empty((k // 512, 16))
    for p in range(k // 512):
        a[p, :8] = np.random.permutation(np.resize(levels, 8))
        for g in range(8):
            far = levels[np.abs(levels - a[p, g]) >= 10]
            a[p, g + 8] = far[np.random.randint(len(far))]
    return np.exp2(a.ravel()).repeat(32)


def f64(x):
    return np.asarray(x).astype(np.float64)


def striped(idx):
    return np.tile(idx.reshape(-1, 16).T, (8, 1)).astype(np.uint16)


def unstriped(offs):
    return offs[:16].T.reshape(-1).astype(np.int64)


def striped8(idx):
    return np.concatenate([x.reshape(-1, 16).T for x in idx]).astype(np.uint16)


def runs(offs, k):
    lists = np.stack([offs[16 * r : 16 * r + 16].T.reshape(-1) for r in range(8)]).astype(np.int64)
    return lists[np.arange(k) % 512 // 64]


def pack_weight(w):
    k, n = w.shape
    w = f64(np.asarray(w, np.float32).astype(ml_dtypes.bfloat16)).reshape(k // 32, 32, n)
    amax = np.abs(w).max(1)
    byte = np.clip(np.where(amax > 0, np.frexp(amax)[1] - 1 + 127 - 7, 1), 1, 254)
    scaled = (w * np.exp2(127.0 - byte)[:, None, :]).reshape(k, n).astype(np.float32)
    words = np.ascontiguousarray(scaled.reshape(k // 512, 128, 4, n).transpose(0, 1, 3, 2)).astype(ml_dtypes.float8_e4m3fn).view(np.uint8)
    return words, np.ascontiguousarray(byte.astype(np.uint8).reshape(k // 512, 16, n))


def unpack_weight(words, scales):
    g, p, n, _ = words.shape
    vals = np.ascontiguousarray(words).view(ml_dtypes.float8_e4m3fn).astype(np.float64) * np.repeat(np.exp2(scales.astype(np.float64) - 127.0), 8, axis=1)[..., None]
    return vals.transpose(0, 1, 3, 2).reshape(g * 512, n)


def sigmoid(v):
    return 1.0 / (1.0 + np.exp(-np.maximum(v, -700.0)))


K, T, S, N, H = 512, 2048, 512, 512, 512


def setup_inputs():
    n = np.random.standard_normal
    s = mx_kscale(K)[:, None]
    u = mx_kscale(H)
    packed_xT = pack_weight(n((K, T)) * s)
    return {
        "x_words": packed_xT[0],
        "x_scales": packed_xT[1],
        "w1": (n((K, H)) / np.sqrt(K) / s).astype(np.float32),
        "gn": (np.random.uniform(0.5, 1.5, (H, 1)) * u[:, None]).astype(np.float32),
        "w2": (n((H, N)) / np.sqrt(H) / u[:, None]).astype(np.float32),
        "offs": striped(np.random.permutation(T)[:S]),
        "n1": striped8(np.stack([np.random.permutation(S) for _ in range(8)])),
        "n2": striped8(np.stack([np.random.permutation(S) for _ in range(8)])),
        "n3": striped8(np.stack([np.random.permutation(S) for _ in range(8)])),
    }


def reference(x_words, x_scales, w1, gn, w2, offs, n1, n2, n3):
    xq = unpack_weight(x_words, x_scales)[:, unstriped(offs)]
    y = mxq(f64(w1), 0, "e4m3").T @ xq
    sq = (y) ** 2
    z = f64(gn) * (np.sqrt(sq + 0.5 * (sq[np.arange(H)[:, None], runs(n1, H)]) + 0.25 * (sq[np.arange(H)[:, None], runs(n2, H)]) + 0.1))
    h = mxq(f64(w2), 0, "e4m3").T @ mxq(z, 0, "e4m3")
    return (h - (h[np.arange(N)[:, None], runs(n3, N)])) * sigmoid(h)

@@ -1,0 +1,224 @@
+import math
+from contextlib import ExitStack
+
+import concourse.mybir as mybir
+
+K, T, S, H, N = 512, 2048, 512, 512, 512
+FLOPS = 2 * K * H * S + 2 * H * N * S
+
+F32 = mybir.dt.float32
+BF16 = mybir.dt.bfloat16
+I32 = mybir.dt.int32
+U32 = mybir.dt.uint32
+U16 = mybir.dt.uint16
+U8 = mybir.dt.uint8
+FP8X4 = mybir.dt.float8_e4m3fn_x4
+ACT = mybir.ActivationFunctionType
+ALU = mybir.AluOpType
+
+P = 128
+PACK = 4
+HALF = 256
+QUARTER = 128
+W1_SPLIT = 48
+
+
+def tile_picked_quadmean_none_p_kernel(tc, x_words, x_scales, w1, gn, w2, offs, n1, n2, n3, out):
+    nc = tc.nc
+    with ExitStack() as ctx:
+        keep = ctx.enter_context(tc.tile_pool(name="keep", bufs=1))
+        psum = ctx.enter_context(tc.psum_pool(name="psum", bufs=1))
+
+        def sb(name, shape, dtype):
+            return keep.tile(shape, dtype, name=name, align_bytes=64)
+
+        offs_t = sb("offs_t", [P, S // 16], U16)
+        n1_t = sb("n1_t", [P, S // 16], U16)
+        n2_t = sb("n2_t", [P, S // 16], U16)
+        n3_t = sb("n3_t", [P, S // 16], U16)
+        xw = sb("xw", [P, T], I32)
+        xs = sb("xs", [P, T], U8)
+        xq_w = sb("xq_w", [P, S], U32)
+        xq_s = sb("xq_s", [P, S], U8)
+        g = sb("g", [P, PACK], F32)
+        w1_raw = [sb(f"w1_raw{c}", [P, PACK, HALF], F32) for c in range(2)]
+        w2_raw = [sb(f"w2_raw{c}", [P, PACK, HALF], F32) for c in range(2)]
+
+        nc.gpsimd.memset(xs[:].bitcast(I32), 0)
+        nc.sync.dma_start(offs_t[:], offs)
+        nc.sync.dma_start(xw[:], x_words[0].rearrange("p n t -> p (n t)").bitcast(I32))
+        for q in range(4):
+            nc.sync.dma_start(xs[32 * q : 32 * q + 4, :].bitcast(I32), x_scales[0, 4 * q : 4 * q + 4, :].bitcast(I32))
+        w1_rows = w1.rearrange("(p j) c -> p j c", j=PACK)
+        w2_rows = w2.rearrange("(p j) c -> p j c", j=PACK)
+        for c in range(2):
+            nc.sync.dma_start(w1_raw[c][:], w1_rows[:, :, c * HALF : (c + 1) * HALF])
+        nc.sync.dma_start(g[:], gn.rearrange("(p t) o -> p (t o)", t=PACK))
+        nc.sync.dma_start(w2_raw[0][:], w2_rows[:, :, 0:HALF])
+        nc.sync.dma_start(n2_t[:], n2)
+        nc.sync.dma_start(n1_t[:], n1)
+        nc.sync.dma_start(w2_raw[1][:], w2_rows[:, :, HALF:N])
+        nc.sync.dma_start(n3_t[:], n3)
+
+        quarter = sb("quarter", [P, 1], F32)
+        tie = sb("tie", [P, 1], F32)
+        nc.gpsimd.memset(quarter[:], 0.25)
+        nc.scalar.activation(tie[:], quarter[:], ACT.Sqrt)
+        g_n2 = sb("g_n2", [P, PACK], F32)
+        g_n1 = sb("g_n1", [P, PACK], F32)
+        g_bias = sb("g_bias", [P, PACK], F32)
+        g_sign0 = sb("g_sign0", [P, PACK], F32)
+        g_sign = sb("g_sign", [P, PACK], F32)
+        nc.scalar.activation(g_sign0[:], g[:], ACT.Sign)
+        nc.scalar.activation(g_n2[:], g[:], ACT.Copy, scale=0.5)
+        nc.scalar.activation(g_n1[:], g[:], ACT.Copy, scale=math.sqrt(0.5))
+        nc.scalar.activation(g_bias[:], g[:], ACT.Square, scale=math.sqrt(0.1))
+        nc.scalar.activation(g_sign[:], g_sign0[:], ACT.Sign, bias=tie[:])
+
+        nc.vector.tensor_copy(xq_w[:], xw[:].bitcast(U32).indirect(offs_t[:]))
+        nc.vector.tensor_copy(xq_s[:], xs[:].indirect(offs_t[:]))
+
+        w1_bf = sb("w1_bf", [P, PACK * H], BF16)
+        w1_codes = sb("w1_codes", [P, H], U32)
+        w1_scales = sb("w1_scales", [P, H], U8)
+        w2_bf = sb("w2_bf", [P, PACK * N], BF16)
+        w2_codes = sb("w2_codes", [P, N], U32)
+        w2_scales = sb("w2_scales", [P, N], U8)
+
+        def dealt(bf, raw, c, m0, m1):
+            dst = bf[:].rearrange("p (t m j) -> p m j t", t=PACK, j=PACK)[:, 64 * c + m0 : 64 * c + m1]
+            src = raw[:].rearrange("p j (m t) -> p m j t", t=PACK)[:, m0:m1]
+            return dst, src
+
+        nc.scalar.copy(*dealt(w1_bf, w1_raw[0], 0, 0, 64))
+        nc.vector.tensor_copy(*dealt(w1_bf, w1_raw[1], 1, 0, W1_SPLIT))
+        nc.scalar.copy(*dealt(w1_bf, w1_raw[1], 1, W1_SPLIT, 64))
+
+        y = [psum.tile([P, S], F32, name=f"y{t}") for t in range(PACK)]
+        h_first = [psum.tile([P, HALF], F32, name=f"h_first{t}") for t in range(PACK)]
+        for t in range(PACK):
+            cols = slice(P * t, P * (t + 1))
+            nc.vector.quantize_mx(w1_codes[:, cols].bitcast(FP8X4), w1_scales[:, cols], w1_bf[:, 4 * P * t : 4 * P * (t + 1)])
+            nc.tensor.matmul_mx(y[t][:], w1_codes[:, cols].bitcast(FP8X4), w1_scales[:, cols], xq_w[:].bitcast(FP8X4), xq_s[:], start=True, stop=True)
+
+        def cast_w2(c):
+            dst, src = dealt(w2_bf, w2_raw[c], c, 0, 64)
+            sign = g_sign[:].unsqueeze(1).unsqueeze(3).to_broadcast([P, 64, PACK, PACK])
+            nc.vector.tensor_tensor(dst, src, sign, ALU.mult)
+
+        cast_w2(0)
+
+        q4 = [sb(f"q4_{t}", [P, S], F32) for t in range(PACK)]
+        q2 = [sb(f"q2_{t}", [P, S], F32) for t in range(PACK)]
+        base = [sb(f"base{t}", [P, S], F32) for t in range(PACK)]
+        for t in range(PACK):
+            nc.scalar.activation(q4[t][:], y[t][:], ACT.Square, scale=g_n2[:, t : t + 1])
+            nc.scalar.activation(q2[t][:], y[t][:], ACT.Square, scale=g_n1[:, t : t + 1])
+            if t == 0:
+                nc.vector.tensor_scalar(base[t][:], q4[t][:], 4.0, g_bias[:, t : t + 1], ALU.mult, ALU.add)
+            else:
+                nc.scalar.activation(base[t][:], q4[t][:], ACT.Identity, scale=4.0, bias=g_bias[:, t : t + 1])
+
+        chunks = [(0, HALF), (HALF, QUARTER), (HALF + QUARTER, QUARTER)]
+        sums = [[sb(f"sums{c}_{pair}", [P, 2, w], F32) for pair in range(2)] for c, (c0, w) in enumerate(chunks)]
+        z_bf = [sb(f"z_bf{c}", [P, PACK * w], BF16) for c, (c0, w) in enumerate(chunks)]
+        z_codes = [sb(f"z_codes{c}", [P, w], U32) for c, (c0, w) in enumerate(chunks)]
+        z_scales = [sb(f"z_scales{c}", [P, w], U8) for c, (c0, w) in enumerate(chunks)]
+        part0 = sb("part0", [P, S], F32)
+        ring = [sb(f"ring{i}", [P, QUARTER], F32) for i in range(3)]
+
+        def entries(lst, a, w):
+            return lst[:, a // 16 : (a + w) // 16]
+
+        def first(t, a, w, part):
+            nc.vector.tensor_tensor(part, q4[t][:].indirect(entries(n2_t, a, w)), base[t][:, a : a + w], ALU.add)
+
+        def second(t, c, a, w, part):
+            lo = a - chunks[c][0]
+            nc.vector.tensor_tensor(sums[c][t // 2][:, t % 2, lo : lo + w], q2[t][:].indirect(entries(n1_t, a, w)), part, ALU.add)
+
+        def root(c, pair):
+            dst = z_bf[c][:].rearrange("p (n t) -> p n t", t=PACK)[:, :, 2 * pair : 2 * pair + 2]
+            nc.scalar.activation(dst, sums[c][pair][:].rearrange("p t n -> p n t"), ACT.Sqrt)
+
+        def h_bank(t, c):
+            if c == 0:
+                return h_first[t][:]
+            return y[t][:, chunks[c][0] - HALF : chunks[c][0] - HALF + chunks[c][1]]
+
+        def second_product(c):
+            nc.vector.quantize_mx(z_codes[c][:].bitcast(FP8X4), z_scales[c][:], z_bf[c][:])
+            for t in range(PACK):
+                cols = slice(P * t, P * (t + 1))
+                nc.tensor.matmul_mx(h_bank(t, c), w2_codes[:, cols].bitcast(FP8X4), w2_scales[:, cols], z_codes[c][:].bitcast(FP8X4), z_scales[c][:], start=True, stop=True)
+
+        for a in (0, HALF):
+            first(0, a, HALF, part0[:, a : a + HALF])
+        for c, (c0, w) in enumerate(chunks):
+            second(0, c, c0, w, part0[:, c0 : c0 + w])
+        k = 0
+        for t in range(1, PACK):
+            for a in (0, QUARTER):
+                first(t, a, QUARTER, ring[(k + a // QUARTER) % 3][:])
+            for a in (0, QUARTER):
+                second(t, 0, a, QUARTER, ring[(k + a // QUARTER) % 3][:])
+            k = k + 2
+            if t == 1:
+                cast_w2(1)
+                root(0, 0)
+            if t == 2:
+                nc.vector.quantize_mx(w2_codes[:].bitcast(FP8X4), w2_scales[:], w2_bf[:])
+        root(0, 1)
+        order = (3, 1, 2)
+        for i, t in enumerate(order):
+            first(t, HALF, QUARTER, ring[i][:])
+        for i, t in enumerate(order):
+            second(t, 1, HALF, QUARTER, ring[i][:])
+        second_product(0)
+        root(1, 0)
+        root(1, 1)
+
+        window = [sb(f"window{t}", [P, S], F32) for t in range(PACK)]
+        plain = [sb(f"plain{t}", [P, S], F32) for t in range(PACK)]
+        gate = [sb(f"gate{t}", [P, S], F32) for t in range(PACK)]
+        diff = [sb(f"diff{t}", [P, S], F32) for t in range(PACK)]
+        res = [sb(f"res{t}", [P, S], F32) for t in range(PACK)]
+        for t in range(2):
+            nc.scalar.copy(window[t][:, 0:HALF], h_first[t][:])
+            nc.scalar.copy(plain[t][:, 0:HALF], h_first[t][:])
+
+        last = chunks[2][0]
+        spent = z_bf[0][:].bitcast(F32)
+        for t in range(1, PACK):
+            first(t, last, QUARTER, spent[:, QUARTER * t : QUARTER * (t + 1)])
+        second_product(1)
+        for t in range(1, PACK):
+            second(t, 2, last, QUARTER, spent[:, QUARTER * t : QUARTER * (t + 1)])
+            if t % 2 == 1:
+                root(2, t // 2)
+        second_product(2)
+
+        nc.vector.tensor_copy(window[0][:, HALF:S], y[0][:, 0:HALF])
+        nc.vector.tensor_copy(plain[0][:, HALF:S], y[0][:, 0:HALF])
+        nc.scalar.copy(window[1][:, HALF:S], y[1][:, 0:HALF])
+        nc.scalar.copy(plain[1][:, HALF:S], y[1][:, 0:HALF])
+        out_rows = out.rearrange("(p t) n -> p t n", t=PACK)
+
+        def finish(t, a, w):
+            nc.vector.scalar_tensor_tensor(res[t][:, a : a + w], diff[t][:, a : a + w], -1.0, gate[t][:, a : a + w], ALU.mult, ALU.mult)
+            nc.sync.dma_start(out_rows[:, t, a : a + w], res[t][:, a : a + w])
+
+        for t in range(PACK):
+            if t >= 2:
+                nc.scalar.copy(window[t][:, 0:HALF], h_first[t][:])
+                nc.scalar.copy(window[t][:, HALF:S], y[t][:, 0:HALF])
+                nc.scalar.copy(plain[t][:, 0:HALF], h_first[t][:])
+                nc.scalar.copy(plain[t][:, HALF:S], y[t][:, 0:HALF])
+            for a in (0, HALF):
+                nc.vector.tensor_tensor(diff[t][:, a : a + HALF], window[t][:].indirect(entries(n3_t, a, HALF)), plain[t][:, a : a + HALF], ALU.subtract)
+            if t >= 1:
+                nc.scalar.activation(gate[t - 1][:], plain[t - 1][:], ACT.Sigmoid)
+                finish(t - 1, 0, S)
+        nc.scalar.activation(gate[3][:], plain[3][:], ACT.Sigmoid)
+        finish(3, 0, HALF)
+        finish(3, HALF, HALF)

@@ -20,7 +20,8 @@ P = 128
 PACK = 4
 HALF = 256
 QUARTER = 128
-W1_SPLIT = 48
+LEAD = 32
+W1_SPLIT = 36
 
 
 def tile_picked_quadmean_none_p_kernel(tc, x_words, x_scales, w1, gn, w2, offs, n1, n2, n3, out):
@@ -45,6 +46,7 @@ def tile_picked_quadmean_none_p_kernel(tc, x_words, x_scales, w1, gn, w2, offs, 
         w2_raw = [sb(f"w2_raw{c}", [P, PACK, HALF], F32) for c in range(2)]
 
         nc.gpsimd.memset(xs[:].bitcast(I32), 0)
+        nc.scalar.dma_start(g[:], gn.rearrange("(p t) o -> p (t o)", t=PACK))
         nc.sync.dma_start(offs_t[:], offs)
         nc.sync.dma_start(xw[:], x_words[0].rearrange("p n t -> p (n t)").bitcast(I32))
         for q in range(4):
@@ -53,11 +55,10 @@ def tile_picked_quadmean_none_p_kernel(tc, x_words, x_scales, w1, gn, w2, offs, 
         w2_rows = w2.rearrange("(p j) c -> p j c", j=PACK)
         for c in range(2):
             nc.sync.dma_start(w1_raw[c][:], w1_rows[:, :, c * HALF : (c + 1) * HALF])
-        nc.sync.dma_start(g[:], gn.rearrange("(p t) o -> p (t o)", t=PACK))
         nc.sync.dma_start(w2_raw[0][:], w2_rows[:, :, 0:HALF])
+        nc.sync.dma_start(w2_raw[1][:], w2_rows[:, :, HALF:N])
         nc.sync.dma_start(n2_t[:], n2)
         nc.sync.dma_start(n1_t[:], n1)
-        nc.sync.dma_start(w2_raw[1][:], w2_rows[:, :, HALF:N])
         nc.sync.dma_start(n3_t[:], n3)
 
         quarter = sb("quarter", [P, 1], F32)
@@ -81,7 +82,6 @@ def tile_picked_quadmean_none_p_kernel(tc, x_words, x_scales, w1, gn, w2, offs, 
         w1_bf = sb("w1_bf", [P, PACK * H], BF16)
         w1_codes = sb("w1_codes", [P, H], U32)
         w1_scales = sb("w1_scales", [P, H], U8)
-        w2_bf = sb("w2_bf", [P, PACK * N], BF16)
         w2_codes = sb("w2_codes", [P, N], U32)
         w2_scales = sb("w2_scales", [P, N], U8)
 
@@ -95,130 +95,167 @@ def tile_picked_quadmean_none_p_kernel(tc, x_words, x_scales, w1, gn, w2, offs, 
         nc.scalar.copy(*dealt(w1_bf, w1_raw[1], 1, W1_SPLIT, 64))
 
         y = [psum.tile([P, S], F32, name=f"y{t}") for t in range(PACK)]
-        h_first = [psum.tile([P, HALF], F32, name=f"h_first{t}") for t in range(PACK)]
+        h = [psum.tile([P, S], F32, name=f"h{t}") for t in range(PACK)]
         for t in range(PACK):
             cols = slice(P * t, P * (t + 1))
             nc.vector.quantize_mx(w1_codes[:, cols].bitcast(FP8X4), w1_scales[:, cols], w1_bf[:, 4 * P * t : 4 * P * (t + 1)])
             nc.tensor.matmul_mx(y[t][:], w1_codes[:, cols].bitcast(FP8X4), w1_scales[:, cols], xq_w[:].bitcast(FP8X4), xq_s[:], start=True, stop=True)
 
-        def cast_w2(c):
-            dst, src = dealt(w2_bf, w2_raw[c], c, 0, 64)
-            sign = g_sign[:].unsqueeze(1).unsqueeze(3).to_broadcast([P, 64, PACK, PACK])
-            nc.vector.tensor_tensor(dst, src, sign, ALU.mult)
-
-        cast_w2(0)
-
         q4 = [sb(f"q4_{t}", [P, S], F32) for t in range(PACK)]
         q2 = [sb(f"q2_{t}", [P, S], F32) for t in range(PACK)]
         base = [sb(f"base{t}", [P, S], F32) for t in range(PACK)]
-        for t in range(PACK):
-            nc.scalar.activation(q4[t][:], y[t][:], ACT.Square, scale=g_n2[:, t : t + 1])
-            nc.scalar.activation(q2[t][:], y[t][:], ACT.Square, scale=g_n1[:, t : t + 1])
-            if t == 0:
-                nc.vector.tensor_scalar(base[t][:], q4[t][:], 4.0, g_bias[:, t : t + 1], ALU.mult, ALU.add)
-            else:
-                nc.scalar.activation(base[t][:], q4[t][:], ACT.Identity, scale=4.0, bias=g_bias[:, t : t + 1])
+        part = [sb(f"part{i}", [P, S], F32) for i in range(3)]
+        w2_bf = [sb("w2_bf", [P, 2 * N], BF16)[:], part[2][:].bitcast(BF16)]
 
-        chunks = [(0, HALF), (HALF, QUARTER), (HALF + QUARTER, QUARTER)]
-        sums = [[sb(f"sums{c}_{pair}", [P, 2, w], F32) for pair in range(2)] for c, (c0, w) in enumerate(chunks)]
-        z_bf = [sb(f"z_bf{c}", [P, PACK * w], BF16) for c, (c0, w) in enumerate(chunks)]
-        z_codes = [sb(f"z_codes{c}", [P, w], U32) for c, (c0, w) in enumerate(chunks)]
-        z_scales = [sb(f"z_scales{c}", [P, w], U8) for c, (c0, w) in enumerate(chunks)]
-        part0 = sb("part0", [P, S], F32)
-        ring = [sb(f"ring{i}", [P, QUARTER], F32) for i in range(3)]
+        def cast_w2(c, pair):
+            dst = w2_bf[pair].rearrange("p (t m j) -> p m j t", t=2, j=PACK)[:, 64 * c : 64 * (c + 1)]
+            src = w2_raw[c][:].rearrange("p j (m t) -> p m j t", t=PACK)[:, :, :, 2 * pair : 2 * pair + 2]
+            sign = g_sign[:].unsqueeze(1).unsqueeze(3).to_broadcast([P, 64, PACK, 2])
+            nc.vector.tensor_tensor(dst, src, sign, ALU.mult)
 
-        def entries(lst, a, w):
-            return lst[:, a // 16 : (a + w) // 16]
+        def quantise_w2(pair):
+            cols = slice(HALF * pair, HALF * (pair + 1))
+            nc.vector.quantize_mx(w2_codes[:, cols].bitcast(FP8X4), w2_scales[:, cols], w2_bf[pair])
 
-        def first(t, a, w, part):
-            nc.vector.tensor_tensor(part, q4[t][:].indirect(entries(n2_t, a, w)), base[t][:, a : a + w], ALU.add)
+        def square(dst, t, scale):
+            nc.scalar.activation(dst[t][:], y[t][:], ACT.Square, scale=scale[:, t : t + 1])
 
-        def second(t, c, a, w, part):
-            lo = a - chunks[c][0]
-            nc.vector.tensor_tensor(sums[c][t // 2][:, t % 2, lo : lo + w], q2[t][:].indirect(entries(n1_t, a, w)), part, ALU.add)
+        def own_term(t):
+            nc.scalar.activation(base[t][:], q4[t][:], ACT.Identity, scale=4.0, bias=g_bias[:, t : t + 1])
 
-        def root(c, pair):
-            dst = z_bf[c][:].rearrange("p (n t) -> p n t", t=PACK)[:, :, 2 * pair : 2 * pair + 2]
-            nc.scalar.activation(dst, sums[c][pair][:].rearrange("p t n -> p n t"), ACT.Sqrt)
+        cast_w2(0, 0)
+        cast_w2(1, 0)
+        square(q4, 0, g_n2)
+        nc.vector.tensor_scalar(base[0][:], q4[0][:], 4.0, g_bias[:, 0:1], ALU.mult, ALU.add)
+        quantise_w2(0)
+        square(q2, 0, g_n1)
+        square(q4, 1, g_n2)
+        square(q2, 1, g_n1)
+        own_term(1)
+        for t in (2, 3):
+            square(q4, t, g_n2)
+        for t in (2, 3):
+            own_term(t)
+        for t in (2, 3):
+            square(q2, t, g_n1)
 
-        def h_bank(t, c):
-            if c == 0:
-                return h_first[t][:]
-            return y[t][:, chunks[c][0] - HALF : chunks[c][0] - HALF + chunks[c][1]]
-
-        def second_product(c):
-            nc.vector.quantize_mx(z_codes[c][:].bitcast(FP8X4), z_scales[c][:], z_bf[c][:])
-            for t in range(PACK):
-                cols = slice(P * t, P * (t + 1))
-                nc.tensor.matmul_mx(h_bank(t, c), w2_codes[:, cols].bitcast(FP8X4), w2_scales[:, cols], z_codes[c][:].bitcast(FP8X4), z_scales[c][:], start=True, stop=True)
-
-        for a in (0, HALF):
-            first(0, a, HALF, part0[:, a : a + HALF])
-        for c, (c0, w) in enumerate(chunks):
-            second(0, c, c0, w, part0[:, c0 : c0 + w])
-        k = 0
-        for t in range(1, PACK):
-            for a in (0, QUARTER):
-                first(t, a, QUARTER, ring[(k + a // QUARTER) % 3][:])
-            for a in (0, QUARTER):
-                second(t, 0, a, QUARTER, ring[(k + a // QUARTER) % 3][:])
-            k = k + 2
-            if t == 1:
-                cast_w2(1)
-                root(0, 0)
-            if t == 2:
-                nc.vector.quantize_mx(w2_codes[:].bitcast(FP8X4), w2_scales[:], w2_bf[:])
-        root(0, 1)
-        order = (3, 1, 2)
-        for i, t in enumerate(order):
-            first(t, HALF, QUARTER, ring[i][:])
-        for i, t in enumerate(order):
-            second(t, 1, HALF, QUARTER, ring[i][:])
-        second_product(0)
-        root(1, 0)
-        root(1, 1)
-
-        window = [sb(f"window{t}", [P, S], F32) for t in range(PACK)]
+        window = [sb(f"window{t}", [P, 2 * S if t in (1, 2) else S], F32) for t in range(PACK)]
+        for t in (1, 2):
+            nc.gpsimd.memset(window[t][:, S : 2 * S], 0.0)
         plain = [sb(f"plain{t}", [P, S], F32) for t in range(PACK)]
         gate = [sb(f"gate{t}", [P, S], F32) for t in range(PACK)]
         diff = [sb(f"diff{t}", [P, S], F32) for t in range(PACK)]
         res = [sb(f"res{t}", [P, S], F32) for t in range(PACK)]
+
+        chunks = [(0, HALF), (HALF, QUARTER), (HALF + QUARTER, QUARTER)]
+        sums01 = sb("sums01", [P, 2 * S], F32)
+        sums23 = [gate[0][:], gate[0][:, HALF:S], gate[0][:, 0:HALF]]
+        z_half = [sb(f"z_half{c}", [P, PACK * HALF], BF16) for c in range(2)]
+        z_codes = [sb(f"z_codes{c}", [P, w], U32) for c, (c0, w) in enumerate(chunks)]
+        z_scales = [sb(f"z_scales{c}", [P, w], U8) for c, (c0, w) in enumerate(chunks)]
+
+        def entries(lst, a, w):
+            return lst[:, a // 16 : (a + w) // 16]
+
+        def first_neighbours(units):
+            for t, a, w, tmp, total in units:
+                nc.vector.tensor_tensor(tmp, q4[t][:].indirect(entries(n2_t, a, w)), base[t][:, a : a + w], ALU.add)
+
+        def second_neighbours(units):
+            for t, a, w, tmp, total in units:
+                nc.vector.tensor_tensor(total, q2[t][:].indirect(entries(n1_t, a, w)), tmp, ALU.add)
+
+        def z_view(a, w):
+            return z_half[a // HALF][:, PACK * (a % HALF) : PACK * (a % HALF + w)]
+
+        def root(src, a, w, pair):
+            dst = z_view(a, w).rearrange("p (n t) -> p n t", t=PACK)[:, :, 2 * pair : 2 * pair + 2]
+            nc.scalar.activation(dst, src, ACT.Sqrt)
+
+        def root01(a, w):
+            root(sums01[:].rearrange("p (t n) -> p n t", t=2)[:, a : a + w, :], a, w, 0)
+
+        def root23(c):
+            root(sums23[c].rearrange("p (t n) -> p n t", t=2), chunks[c][0], chunks[c][1], 1)
+
+        def h_bank(t, a, w):
+            if t == 0 and a == HALF + QUARTER:
+                return y[2][:, 0:w]
+            if t == 0 and a >= HALF:
+                return y[t][:, a - HALF : a - HALF + w]
+            return h[t][:, a : a + w]
+
+        def quantise(c):
+            nc.vector.quantize_mx(z_codes[c][:].bitcast(FP8X4), z_scales[c][:], z_view(*chunks[c]))
+
+        def second_product(c, tiles):
+            for t in tiles:
+                cols = slice(P * t, P * (t + 1))
+                nc.tensor.matmul_mx(h_bank(t, *chunks[c]), w2_codes[:, cols].bitcast(FP8X4), w2_scales[:, cols], z_codes[c][:].bitcast(FP8X4), z_scales[c][:], start=True, stop=True)
+
         for t in range(2):
-            nc.scalar.copy(window[t][:, 0:HALF], h_first[t][:])
-            nc.scalar.copy(plain[t][:, 0:HALF], h_first[t][:])
+            units = [(t, a, HALF, part[t][:, a : a + HALF], sums01[:, S * t + a : S * t + a + HALF]) for a in (0, HALF)]
+            first_neighbours(units)
+            second_neighbours(units)
+        root01(0, HALF)
+        root01(HALF, HALF)
 
-        last = chunks[2][0]
-        spent = z_bf[0][:].bitcast(F32)
-        for t in range(1, PACK):
-            first(t, last, QUARTER, spent[:, QUARTER * t : QUARTER * (t + 1)])
-        second_product(1)
-        for t in range(1, PACK):
-            second(t, 2, last, QUARTER, spent[:, QUARTER * t : QUARTER * (t + 1)])
-            if t % 2 == 1:
-                root(2, t // 2)
-        second_product(2)
+        early = [(2, 0, HALF, part[0][:, 0:HALF], sums23[0][:, 0:HALF]), (3, 0, HALF, part[2][:, QUARTER : QUARTER + HALF], sums23[0][:, HALF:S])]
+        first_neighbours(early)
+        second_neighbours(early)
+        root23(0)
+        late = [(t, HALF, HALF, part[2][:, HALF * (t - 2) : HALF * (t - 1)], None) for t in (2, 3)]
+        first_neighbours(late)
+        quantise(0)
+        second_product(0, (0, 1))
+        for c in (1, 2):
+            a, w = chunks[c]
+            second_neighbours([(t, a, w, tmp[:, a - HALF : a - HALF + w], sums23[c][:, w * (t - 2) : w * (t - 1)]) for t, a0, w0, tmp, total in late])
+            if c == 1:
+                nc.scalar.copy(window[0][:, 0:HALF], h[0][:, 0:HALF])
+                nc.scalar.copy(plain[0][:, 0:HALF], h[0][:, 0:HALF])
+            root23(c)
+        quantise(1)
+        second_product(1, (0, 1))
+        nc.scalar.activation(gate[0][:, 0:LEAD], plain[0][:, 0:LEAD], ACT.Sigmoid)
+        quantise(2)
+        second_product(2, (0, 1))
+        for a, w in chunks[1:]:
+            nc.vector.tensor_copy(window[0][:, a : a + w], h_bank(0, a, w))
+            nc.vector.tensor_copy(plain[0][:, a : a + w], h_bank(0, a, w))
+        cast_w2(0, 1)
+        cast_w2(1, 1)
+        quantise_w2(1)
+        for t in (2, 3):
+            for c in range(3):
+                second_product(c, (t,))
 
-        nc.vector.tensor_copy(window[0][:, HALF:S], y[0][:, 0:HALF])
-        nc.vector.tensor_copy(plain[0][:, HALF:S], y[0][:, 0:HALF])
-        nc.scalar.copy(window[1][:, HALF:S], y[1][:, 0:HALF])
-        nc.scalar.copy(plain[1][:, HALF:S], y[1][:, 0:HALF])
         out_rows = out.rearrange("(p t) n -> p t n", t=PACK)
+
+        def gather(t, a, w):
+            nc.vector.tensor_tensor(diff[t][:, a : a + w], window[t][:].indirect(entries(n3_t, a, w)), plain[t][:, a : a + w], ALU.subtract)
 
         def finish(t, a, w):
             nc.vector.scalar_tensor_tensor(res[t][:, a : a + w], diff[t][:, a : a + w], -1.0, gate[t][:, a : a + w], ALU.mult, ALU.mult)
             nc.sync.dma_start(out_rows[:, t, a : a + w], res[t][:, a : a + w])
 
-        for t in range(PACK):
-            if t >= 2:
-                nc.scalar.copy(window[t][:, 0:HALF], h_first[t][:])
-                nc.scalar.copy(window[t][:, HALF:S], y[t][:, 0:HALF])
-                nc.scalar.copy(plain[t][:, 0:HALF], h_first[t][:])
-                nc.scalar.copy(plain[t][:, HALF:S], y[t][:, 0:HALF])
-            for a in (0, HALF):
-                nc.vector.tensor_tensor(diff[t][:, a : a + HALF], window[t][:].indirect(entries(n3_t, a, HALF)), plain[t][:, a : a + HALF], ALU.subtract)
-            if t >= 1:
-                nc.scalar.activation(gate[t - 1][:], plain[t - 1][:], ACT.Sigmoid)
-                finish(t - 1, 0, S)
+        gather(0, 0, HALF)
+        gather(0, HALF, HALF)
+        for t in range(1, PACK):
+            a = 0
+            if t == 3:
+                nc.scalar.activation(gate[2][:], plain[2][:], ACT.Sigmoid)
+                finish(2, 0, S)
+            nc.scalar.copy(window[t][:, a:S], h_bank(t, a, S - a))
+            nc.scalar.copy(plain[t][:, a:S], h_bank(t, a, S - a))
+            if t == 3:
+                break
+            gather(t, 0, S)
+            a = LEAD if t == 1 else 0
+            nc.scalar.activation(gate[t - 1][:, a:S], plain[t - 1][:, a:S], ACT.Sigmoid)
+            finish(t - 1, 0, S)
+        gather(3, 0, HALF)
+        gather(3, HALF, HALF)
         nc.scalar.activation(gate[3][:], plain[3][:], ACT.Sigmoid)
         finish(3, 0, HALF)
         finish(3, HALF, HALF)

@@ -95,39 +95,47 @@ def tile_picked_quadmean_none_p_kernel(tc, x_words, x_scales, w1, gn, w2, offs, 
         nc.scalar.copy(*dealt(w1_bf, w1_raw[1], 1, W1_SPLIT, 64))
 
         y = [psum.tile([P, S], F32, name=f"y{t}") for t in range(PACK)]
-        h = [psum.tile([P, S], F32, name=f"h{t}") for t in range(PACK)]
+        y0_late = psum.tile([P, HALF], F32, name="y0_late")
+        h = [psum.tile([P, S], F32, name=f"h{t}") for t in range(3)] + [y[1]]
         for t in range(PACK):
             cols = slice(P * t, P * (t + 1))
             nc.vector.quantize_mx(w1_codes[:, cols].bitcast(FP8X4), w1_scales[:, cols], w1_bf[:, 4 * P * t : 4 * P * (t + 1)])
-            nc.tensor.matmul_mx(y[t][:], w1_codes[:, cols].bitcast(FP8X4), w1_scales[:, cols], xq_w[:].bitcast(FP8X4), xq_s[:], start=True, stop=True)
+            pieces = [(y[0][:, 0:HALF], 0, HALF), (y0_late[:], HALF, S)] if t == 0 else [(y[t][:], 0, S)]
+            for bank, a, b in pieces:
+                nc.tensor.matmul_mx(bank, w1_codes[:, cols].bitcast(FP8X4), w1_scales[:, cols], xq_w[:, a:b].bitcast(FP8X4), xq_s[:, a:b], start=True, stop=True)
 
         q4 = [sb(f"q4_{t}", [P, S], F32) for t in range(PACK)]
         q2 = [sb(f"q2_{t}", [P, S], F32) for t in range(PACK)]
         base = [sb(f"base{t}", [P, S], F32) for t in range(PACK)]
         part = [sb(f"part{i}", [P, S], F32) for i in range(3)]
-        w2_bf = [sb("w2_bf", [P, 2 * N], BF16)[:], part[2][:].bitcast(BF16)]
+        w2_signed = sb("w2_signed", [P, PACK, N], BF16)
+        w2_bf = [sb(f"w2_bf{pair}", [P, 2 * N], BF16)[:] for pair in range(2)]
 
-        def cast_w2(c, pair):
-            dst = w2_bf[pair].rearrange("p (t m j) -> p m j t", t=2, j=PACK)[:, 64 * c : 64 * (c + 1)]
-            src = w2_raw[c][:].rearrange("p j (m t) -> p m j t", t=PACK)[:, :, :, 2 * pair : 2 * pair + 2]
-            sign = g_sign[:].unsqueeze(1).unsqueeze(3).to_broadcast([P, 64, PACK, 2])
-            nc.vector.tensor_tensor(dst, src, sign, ALU.mult)
+        def sign_w2(c, rows):
+            for j in rows:
+                nc.vector.tensor_scalar(w2_signed[:, j, HALF * c : HALF * (c + 1)], w2_raw[c][:, j, :], g_sign[:, j : j + 1], None, ALU.mult)
+
+        def deal_w2(pair):
+            src = w2_signed[:].rearrange("p j (m t) -> p t m j", t=PACK)[:, 2 * pair : 2 * pair + 2]
+            nc.scalar.copy(w2_bf[pair].rearrange("p (t m j) -> p t m j", t=2, j=PACK), src)
 
         def quantise_w2(pair):
             cols = slice(HALF * pair, HALF * (pair + 1))
             nc.vector.quantize_mx(w2_codes[:, cols].bitcast(FP8X4), w2_scales[:, cols], w2_bf[pair])
 
         def square(dst, t, scale):
-            nc.scalar.activation(dst[t][:], y[t][:], ACT.Square, scale=scale[:, t : t + 1])
+            pieces = [(y[0][:, 0:HALF], 0, HALF), (y0_late[:], HALF, S)] if t == 0 else [(y[t][:], 0, S)]
+            for bank, a, b in pieces:
+                nc.scalar.activation(dst[t][:, a:b], bank, ACT.Square, scale=scale[:, t : t + 1])
 
         def own_term(t):
             nc.scalar.activation(base[t][:], q4[t][:], ACT.Identity, scale=4.0, bias=g_bias[:, t : t + 1])
 
-        cast_w2(0, 0)
-        cast_w2(1, 0)
+        sign_w2(0, range(PACK))
         square(q4, 0, g_n2)
-        nc.vector.tensor_scalar(base[0][:], q4[0][:], 4.0, g_bias[:, 0:1], ALU.mult, ALU.add)
-        quantise_w2(0)
+        for a in (0, HALF):
+            nc.vector.tensor_scalar(base[0][:, a : a + HALF], q4[0][:, a : a + HALF], 4.0, g_bias[:, 0:1], ALU.mult, ALU.add)
+        sign_w2(1, range(2))
         square(q2, 0, g_n1)
         square(q4, 1, g_n2)
         square(q2, 1, g_n1)
@@ -151,8 +159,8 @@ def tile_picked_quadmean_none_p_kernel(tc, x_words, x_scales, w1, gn, w2, offs, 
         sums01 = sb("sums01", [P, 2 * S], F32)
         sums23 = [gate[0][:], gate[0][:, HALF:S], gate[0][:, 0:HALF]]
         z_half = [sb(f"z_half{c}", [P, PACK * HALF], BF16) for c in range(2)]
-        z_codes = [sb(f"z_codes{c}", [P, w], U32) for c, (c0, w) in enumerate(chunks)]
-        z_scales = [sb(f"z_scales{c}", [P, w], U8) for c, (c0, w) in enumerate(chunks)]
+        z_codes = [sb(f"z_codes{c}", [P, HALF], U32) for c in range(2)]
+        z_scales = [sb(f"z_scales{c}", [P, HALF], U8) for c in range(2)]
 
         def entries(lst, a, w):
             return lst[:, a // 16 : (a + w) // 16]
@@ -185,29 +193,38 @@ def tile_picked_quadmean_none_p_kernel(tc, x_words, x_scales, w1, gn, w2, offs, 
                 return y[t][:, a - HALF : a - HALF + w]
             return h[t][:, a : a + w]
 
-        def quantise(c):
-            nc.vector.quantize_mx(z_codes[c][:].bitcast(FP8X4), z_scales[c][:], z_view(*chunks[c]))
+        def z_planes(a, w):
+            cols = slice(a % HALF, a % HALF + w)
+            return z_codes[a // HALF][:, cols].bitcast(FP8X4), z_scales[a // HALF][:, cols]
 
-        def second_product(c, tiles):
-            for t in tiles:
-                cols = slice(P * t, P * (t + 1))
-                nc.tensor.matmul_mx(h_bank(t, *chunks[c]), w2_codes[:, cols].bitcast(FP8X4), w2_scales[:, cols], z_codes[c][:].bitcast(FP8X4), z_scales[c][:], start=True, stop=True)
+        def quantise(c):
+            nc.vector.quantize_mx(*z_planes(*chunks[c]), z_view(*chunks[c]))
+
+        def second_product(t, a, w):
+            cols = slice(P * t, P * (t + 1))
+            nc.tensor.matmul_mx(h_bank(t, a, w), w2_codes[:, cols].bitcast(FP8X4), w2_scales[:, cols], *z_planes(a, w), start=True, stop=True)
 
         for t in range(2):
             units = [(t, a, HALF, part[t][:, a : a + HALF], sums01[:, S * t + a : S * t + a + HALF]) for a in (0, HALF)]
             first_neighbours(units)
             second_neighbours(units)
+        for j in range(2, PACK):
+            nc.scalar.activation(w2_signed[:, j, HALF:N], w2_raw[1][:, j, :], ACT.Copy, scale=g_sign[:, j : j + 1])
         root01(0, HALF)
         root01(HALF, HALF)
+        deal_w2(0)
 
         early = [(2, 0, HALF, part[0][:, 0:HALF], sums23[0][:, 0:HALF]), (3, 0, HALF, part[2][:, QUARTER : QUARTER + HALF], sums23[0][:, HALF:S])]
         first_neighbours(early)
         second_neighbours(early)
         root23(0)
+        deal_w2(1)
         late = [(t, HALF, HALF, part[2][:, HALF * (t - 2) : HALF * (t - 1)], None) for t in (2, 3)]
         first_neighbours(late)
+        quantise_w2(0)
         quantise(0)
-        second_product(0, (0, 1))
+        second_product(0, 0, HALF)
+        second_product(1, 0, HALF)
         for c in (1, 2):
             a, w = chunks[c]
             second_neighbours([(t, a, w, tmp[:, a - HALF : a - HALF + w], sums23[c][:, w * (t - 2) : w * (t - 1)]) for t, a0, w0, tmp, total in late])
@@ -216,19 +233,19 @@ def tile_picked_quadmean_none_p_kernel(tc, x_words, x_scales, w1, gn, w2, offs, 
                 nc.scalar.copy(plain[0][:, 0:HALF], h[0][:, 0:HALF])
             root23(c)
         quantise(1)
-        second_product(1, (0, 1))
+        second_product(0, *chunks[1])
         nc.scalar.activation(gate[0][:, 0:LEAD], plain[0][:, 0:LEAD], ACT.Sigmoid)
         quantise(2)
-        second_product(2, (0, 1))
+        second_product(0, *chunks[2])
         for a, w in chunks[1:]:
             nc.vector.tensor_copy(window[0][:, a : a + w], h_bank(0, a, w))
             nc.vector.tensor_copy(plain[0][:, a : a + w], h_bank(0, a, w))
-        cast_w2(0, 1)
-        cast_w2(1, 1)
         quantise_w2(1)
+        nc.vector.tensor_copy(window[1][:, 0:HALF], h[1][:, 0:HALF])
+        second_product(1, HALF, HALF)
         for t in (2, 3):
-            for c in range(3):
-                second_product(c, (t,))
+            for a in (0, HALF):
+                second_product(t, a, HALF)
 
         out_rows = out.rearrange("(p t) n -> p t n", t=PACK)
 
@@ -242,12 +259,12 @@ def tile_picked_quadmean_none_p_kernel(tc, x_words, x_scales, w1, gn, w2, offs, 
         gather(0, 0, HALF)
         gather(0, HALF, HALF)
         for t in range(1, PACK):
-            a = 0
+            a = HALF if t == 1 else 0
             if t == 3:
                 nc.scalar.activation(gate[2][:], plain[2][:], ACT.Sigmoid)
                 finish(2, 0, S)
             nc.scalar.copy(window[t][:, a:S], h_bank(t, a, S - a))
-            nc.scalar.copy(plain[t][:, a:S], h_bank(t, a, S - a))
+            nc.scalar.copy(plain[t][:], h_bank(t, 0, S))
             if t == 3:
                 break
             gather(t, 0, S)

@@ -18,10 +18,15 @@ ALU = mybir.AluOpType
 
 P = 128
 PACK = 4
+LIST_ROWS = 16
 HALF = 256
 QUARTER = 128
+GROUPS = HALF // PACK
+RUN = 4
+W1_ON_VECTOR = 36
 LEAD = 32
-W1_SPLIT = 36
+
+EARLY, MIDDLE, LAST = (0, HALF), (HALF + QUARTER, QUARTER), (HALF, QUARTER)
 
 
 def tile_picked_quadmean_none_p_kernel(tc, x_words, x_scales, w1, gn, w2, offs, n1, n2, n3, out):
@@ -33,215 +38,189 @@ def tile_picked_quadmean_none_p_kernel(tc, x_words, x_scales, w1, gn, w2, offs, 
         def sb(name, shape, dtype):
             return keep.tile(shape, dtype, name=name, align_bytes=64)
 
-        offs_t = sb("offs_t", [P, S // 16], U16)
-        n1_t = sb("n1_t", [P, S // 16], U16)
-        n2_t = sb("n2_t", [P, S // 16], U16)
-        n3_t = sb("n3_t", [P, S // 16], U16)
-        xw = sb("xw", [P, T], I32)
-        xs = sb("xs", [P, T], U8)
-        xq_w = sb("xq_w", [P, S], U32)
-        xq_s = sb("xq_s", [P, S], U8)
-        g = sb("g", [P, PACK], F32)
+        def entries(list_tile, a, w):
+            return list_tile[:, a // LIST_ROWS : (a + w) // LIST_ROWS]
+
+        offs_tile, n1_tile, n2_tile, n3_tile = [sb(name, [P, S // LIST_ROWS], U16) for name in ("offs_tile", "n1_tile", "n2_tile", "n3_tile")]
+        table_words = sb("table_words", [P, T], I32)
+        table_scales = sb("table_scales", [P, T], U8)
+        gain = sb("gain", [P, PACK], F32)
         w1_raw = [sb(f"w1_raw{c}", [P, PACK, HALF], F32) for c in range(2)]
         w2_raw = [sb(f"w2_raw{c}", [P, PACK, HALF], F32) for c in range(2)]
 
-        nc.gpsimd.memset(xs[:].bitcast(I32), 0)
-        nc.scalar.dma_start(g[:], gn.rearrange("(p t) o -> p (t o)", t=PACK))
-        nc.sync.dma_start(offs_t[:], offs)
-        nc.sync.dma_start(xw[:], x_words[0].rearrange("p n t -> p (n t)").bitcast(I32))
+        nc.gpsimd.memset(table_scales[:].bitcast(I32), 0)
+        nc.scalar.dma_start(gain[:], gn.rearrange("(p t) o -> p (t o)", t=PACK))
+        nc.sync.dma_start(offs_tile[:], offs)
+        nc.sync.dma_start(table_words[:], x_words[0].rearrange("p n j -> p (n j)").bitcast(I32))
         for q in range(4):
-            nc.sync.dma_start(xs[32 * q : 32 * q + 4, :].bitcast(I32), x_scales[0, 4 * q : 4 * q + 4, :].bitcast(I32))
-        w1_rows = w1.rearrange("(p j) c -> p j c", j=PACK)
-        w2_rows = w2.rearrange("(p j) c -> p j c", j=PACK)
-        for c in range(2):
-            nc.sync.dma_start(w1_raw[c][:], w1_rows[:, :, c * HALF : (c + 1) * HALF])
-        nc.sync.dma_start(w2_raw[0][:], w2_rows[:, :, 0:HALF])
-        nc.sync.dma_start(w2_raw[1][:], w2_rows[:, :, HALF:N])
-        nc.sync.dma_start(n2_t[:], n2)
-        nc.sync.dma_start(n1_t[:], n1)
-        nc.sync.dma_start(n3_t[:], n3)
+            nc.sync.dma_start(table_scales[32 * q : 32 * q + 4, :].bitcast(I32), x_scales[0, 4 * q : 4 * q + 4, :].bitcast(I32))
+        for raw, weight in ((w1_raw, w1), (w2_raw, w2)):
+            for c in range(2):
+                nc.sync.dma_start(raw[c][:], weight.rearrange("(p j) n -> p j n", j=PACK)[:, :, HALF * c : HALF * (c + 1)])
+        for list_tile, source in ((n2_tile, n2), (n1_tile, n1), (n3_tile, n3)):
+            nc.sync.dma_start(list_tile[:], source)
 
-        quarter = sb("quarter", [P, 1], F32)
-        tie = sb("tie", [P, 1], F32)
-        nc.gpsimd.memset(quarter[:], 0.25)
-        nc.scalar.activation(tie[:], quarter[:], ACT.Sqrt)
-        g_n2 = sb("g_n2", [P, PACK], F32)
-        g_n1 = sb("g_n1", [P, PACK], F32)
-        g_bias = sb("g_bias", [P, PACK], F32)
-        g_sign0 = sb("g_sign0", [P, PACK], F32)
-        g_sign = sb("g_sign", [P, PACK], F32)
-        nc.scalar.activation(g_sign0[:], g[:], ACT.Sign)
-        nc.scalar.activation(g_n2[:], g[:], ACT.Copy, scale=0.5)
-        nc.scalar.activation(g_n1[:], g[:], ACT.Copy, scale=math.sqrt(0.5))
-        nc.scalar.activation(g_bias[:], g[:], ACT.Square, scale=math.sqrt(0.1))
-        nc.scalar.activation(g_sign[:], g_sign0[:], ACT.Sign, bias=tie[:])
+        one_quarter = sb("one_quarter", [P, 1], F32)
+        one_half = sb("one_half", [P, 1], F32)
+        nc.gpsimd.memset(one_quarter[:], 0.25)
+        nc.scalar.activation(one_half[:], one_quarter[:], ACT.Sqrt)
+        scale_n2, scale_n1, bias_own, sign_or_zero, sign = [sb(name, [P, PACK], F32) for name in ("scale_n2", "scale_n1", "bias_own", "sign_or_zero", "sign")]
+        nc.scalar.activation(sign_or_zero[:], gain[:], ACT.Sign)
+        nc.scalar.activation(scale_n2[:], gain[:], ACT.Copy, scale=0.5)
+        nc.scalar.activation(scale_n1[:], gain[:], ACT.Copy, scale=math.sqrt(0.5))
+        nc.scalar.activation(bias_own[:], gain[:], ACT.Square, scale=math.sqrt(0.1))
+        nc.scalar.activation(sign[:], sign_or_zero[:], ACT.Sign, bias=one_half[:])
 
-        nc.vector.tensor_copy(xq_w[:], xw[:].bitcast(U32).indirect(offs_t[:]))
-        nc.vector.tensor_copy(xq_s[:], xs[:].indirect(offs_t[:]))
+        x_codes = sb("x_codes", [P, S], U32)
+        x_bytes = sb("x_bytes", [P, S], U8)
+        nc.vector.tensor_copy(x_codes[:], table_words[:].bitcast(U32).indirect(offs_tile[:]))
+        nc.vector.tensor_copy(x_bytes[:], table_scales[:].indirect(offs_tile[:]))
 
-        w1_bf = sb("w1_bf", [P, PACK * H], BF16)
+        w1_dealt = sb("w1_dealt", [P, PACK * H], BF16)
         w1_codes = sb("w1_codes", [P, H], U32)
         w1_scales = sb("w1_scales", [P, H], U8)
-        w2_codes = sb("w2_codes", [P, N], U32)
-        w2_scales = sb("w2_scales", [P, N], U8)
 
-        def dealt(bf, raw, c, m0, m1):
-            dst = bf[:].rearrange("p (t m j) -> p m j t", t=PACK, j=PACK)[:, 64 * c + m0 : 64 * c + m1]
-            src = raw[:].rearrange("p j (m t) -> p m j t", t=PACK)[:, m0:m1]
-            return dst, src
+        def deal_w1(copy, c, m0, m1):
+            dst = w1_dealt[:].rearrange("p (t m j) -> p m j t", t=PACK, j=PACK)[:, GROUPS * c + m0 : GROUPS * c + m1]
+            copy(dst, w1_raw[c][:].rearrange("p j (m t) -> p m j t", t=PACK)[:, m0:m1])
 
-        nc.scalar.copy(*dealt(w1_bf, w1_raw[0], 0, 0, 64))
-        nc.vector.tensor_copy(*dealt(w1_bf, w1_raw[1], 1, 0, W1_SPLIT))
-        nc.scalar.copy(*dealt(w1_bf, w1_raw[1], 1, W1_SPLIT, 64))
+        deal_w1(nc.scalar.copy, 0, 0, GROUPS)
+        deal_w1(nc.vector.tensor_copy, 1, 0, W1_ON_VECTOR)
+        deal_w1(nc.scalar.copy, 1, W1_ON_VECTOR, GROUPS)
 
-        y = [psum.tile([P, S], F32, name=f"y{t}") for t in range(PACK)]
-        y0_late = psum.tile([P, HALF], F32, name="y0_late")
-        h = [psum.tile([P, S], F32, name=f"h{t}") for t in range(3)] + [y[1]]
+        bank = [psum.tile([P, S], F32, name=f"bank{b}") for b in range(8)]
+        y_pieces = [[(bank[0][:, 0:HALF], 0, HALF), (bank[4][:, 0:HALF], HALF, S)]] + [[(bank[t][:], 0, S)] for t in range(1, PACK)]
         for t in range(PACK):
             cols = slice(P * t, P * (t + 1))
-            nc.vector.quantize_mx(w1_codes[:, cols].bitcast(FP8X4), w1_scales[:, cols], w1_bf[:, 4 * P * t : 4 * P * (t + 1)])
-            pieces = [(y[0][:, 0:HALF], 0, HALF), (y0_late[:], HALF, S)] if t == 0 else [(y[t][:], 0, S)]
-            for bank, a, b in pieces:
-                nc.tensor.matmul_mx(bank, w1_codes[:, cols].bitcast(FP8X4), w1_scales[:, cols], xq_w[:, a:b].bitcast(FP8X4), xq_s[:, a:b], start=True, stop=True)
+            nc.vector.quantize_mx(w1_codes[:, cols].bitcast(FP8X4), w1_scales[:, cols], w1_dealt[:, PACK * P * t : PACK * P * (t + 1)])
+            for piece, a, b in y_pieces[t]:
+                nc.tensor.matmul_mx(piece, w1_codes[:, cols].bitcast(FP8X4), w1_scales[:, cols], x_codes[:, a:b].bitcast(FP8X4), x_bytes[:, a:b], start=True, stop=True)
 
-        q4 = [sb(f"q4_{t}", [P, S], F32) for t in range(PACK)]
-        q2 = [sb(f"q2_{t}", [P, S], F32) for t in range(PACK)]
-        base = [sb(f"base{t}", [P, S], F32) for t in range(PACK)]
-        part = [sb(f"part{i}", [P, S], F32) for i in range(3)]
+        term_n2 = [sb(f"term_n2_{t}", [P, S], F32) for t in range(PACK)]
+        term_n1 = [sb(f"term_n1_{t}", [P, S], F32) for t in range(PACK)]
+        term_own = [sb(f"term_own{t}", [P, S], F32) for t in range(PACK)]
         w2_signed = sb("w2_signed", [P, PACK, N], BF16)
-        w2_bf = [sb(f"w2_bf{pair}", [P, 2 * N], BF16)[:] for pair in range(2)]
 
-        def sign_w2(c, rows):
-            for j in rows:
-                nc.vector.tensor_scalar(w2_signed[:, j, HALF * c : HALF * (c + 1)], w2_raw[c][:, j, :], g_sign[:, j : j + 1], None, ALU.mult)
+        def square(term, t, scale):
+            for piece, a, b in y_pieces[t]:
+                nc.scalar.activation(term[t][:, a:b], piece, ACT.Square, scale=scale[:, t : t + 1])
 
-        def deal_w2(pair):
-            src = w2_signed[:].rearrange("p j (m t) -> p t m j", t=PACK)[:, 2 * pair : 2 * pair + 2]
-            nc.scalar.copy(w2_bf[pair].rearrange("p (t m j) -> p t m j", t=2, j=PACK), src)
+        def own(t):
+            nc.scalar.activation(term_own[t][:], term_n2[t][:], ACT.Identity, scale=4.0, bias=bias_own[:, t : t + 1])
 
-        def quantise_w2(pair):
-            cols = slice(HALF * pair, HALF * (pair + 1))
-            nc.vector.quantize_mx(w2_codes[:, cols].bitcast(FP8X4), w2_scales[:, cols], w2_bf[pair])
-
-        def square(dst, t, scale):
-            pieces = [(y[0][:, 0:HALF], 0, HALF), (y0_late[:], HALF, S)] if t == 0 else [(y[t][:], 0, S)]
-            for bank, a, b in pieces:
-                nc.scalar.activation(dst[t][:, a:b], bank, ACT.Square, scale=scale[:, t : t + 1])
-
-        def own_term(t):
-            nc.scalar.activation(base[t][:], q4[t][:], ACT.Identity, scale=4.0, bias=g_bias[:, t : t + 1])
-
-        sign_w2(0, range(PACK))
-        square(q4, 0, g_n2)
+        for j in range(PACK):
+            nc.vector.tensor_scalar(w2_signed[:, j, 0:HALF], w2_raw[0][:, j, :], sign[:, j : j + 1], None, ALU.mult)
+        square(term_n2, 0, scale_n2)
         for a in (0, HALF):
-            nc.vector.tensor_scalar(base[0][:, a : a + HALF], q4[0][:, a : a + HALF], 4.0, g_bias[:, 0:1], ALU.mult, ALU.add)
-        sign_w2(1, range(2))
-        square(q2, 0, g_n1)
-        square(q4, 1, g_n2)
-        square(q2, 1, g_n1)
-        own_term(1)
+            nc.vector.tensor_scalar(term_own[0][:, a : a + HALF], term_n2[0][:, a : a + HALF], 4.0, bias_own[:, 0:1], ALU.mult, ALU.add)
+        square(term_n1, 0, scale_n1)
+        square(term_n2, 1, scale_n2)
+        square(term_n1, 1, scale_n1)
+        own(1)
         for t in (2, 3):
-            square(q4, t, g_n2)
+            square(term_n2, t, scale_n2)
         for t in (2, 3):
-            own_term(t)
+            own(t)
+        for j in range(PACK):
+            nc.scalar.activation(w2_signed[:, j, HALF:N], w2_raw[1][:, j, :], ACT.Copy, scale=sign[:, j : j + 1])
         for t in (2, 3):
-            square(q2, t, g_n1)
+            square(term_n1, t, scale_n1)
 
-        window = [sb(f"window{t}", [P, 2 * S if t in (1, 2) else S], F32) for t in range(PACK)]
+        h_window = [sb(f"h_window{t}", [P, 2 * S if t in (1, 2) else S], F32) for t in range(PACK)]
         for t in (1, 2):
-            nc.gpsimd.memset(window[t][:, S : 2 * S], 0.0)
-        plain = [sb(f"plain{t}", [P, S], F32) for t in range(PACK)]
-        gate = [sb(f"gate{t}", [P, S], F32) for t in range(PACK)]
-        diff = [sb(f"diff{t}", [P, S], F32) for t in range(PACK)]
-        res = [sb(f"res{t}", [P, S], F32) for t in range(PACK)]
+            nc.gpsimd.memset(h_window[t][:, S : 2 * S], 0.0)
+        h_plain = [sb(f"h_plain{t}", [P, S], F32) for t in range(PACK)]
 
-        chunks = [(0, HALF), (HALF, QUARTER), (HALF + QUARTER, QUARTER)]
-        sums01 = sb("sums01", [P, 2 * S], F32)
-        sums23 = [gate[0][:], gate[0][:, HALF:S], gate[0][:, 0:HALF]]
+        sums = sb("sums", [P, 6 * HALF], F32)
+        gate = [sums[:, 2 * HALF : 4 * HALF]] + [sb(f"gate{t}", [P, S], F32)[:] for t in range(1, PACK)]
+        partial = [sb(f"partial{i}", [P, S], F32) for i in range(3)]
+        diff = [sb(f"diff{t}", [P, S], F32) for t in range(PACK)]
+        result = [sb(f"result{t}", [P, S], F32) for t in range(PACK)]
         z_half = [sb(f"z_half{c}", [P, PACK * HALF], BF16) for c in range(2)]
         z_codes = [sb(f"z_codes{c}", [P, HALF], U32) for c in range(2)]
         z_scales = [sb(f"z_scales{c}", [P, HALF], U8) for c in range(2)]
+        w2_dealt = [sb(f"w2_dealt{pair}", [P, 2 * N], BF16) for pair in range(2)]
+        w2_codes = sb("w2_codes", [P, N], U32)
+        w2_scales = sb("w2_scales", [P, N], U8)
 
-        def entries(lst, a, w):
-            return lst[:, a // 16 : (a + w) // 16]
+        def sum_rows(a, w):
+            first_row = 2 if a < HALF else 0
+            rows = sums[:, first_row * HALF : (first_row + PACK) * HALF].rearrange("p (t n) -> p t n", t=PACK)
+            return rows[:, :, a % HALF : a % HALF + w]
 
-        def first_neighbours(units):
-            for t, a, w, tmp, total in units:
-                nc.vector.tensor_tensor(tmp, q4[t][:].indirect(entries(n2_t, a, w)), base[t][:, a : a + w], ALU.add)
+        def add_n2(t, a, w, held):
+            nc.vector.tensor_tensor(held, term_n2[t][:].indirect(entries(n2_tile, a, w)), term_own[t][:, a : a + w], ALU.add)
 
-        def second_neighbours(units):
-            for t, a, w, tmp, total in units:
-                nc.vector.tensor_tensor(total, q2[t][:].indirect(entries(n1_t, a, w)), tmp, ALU.add)
+        def add_n1(t, a, w, held):
+            nc.vector.tensor_tensor(sum_rows(a, w)[:, t], term_n1[t][:].indirect(entries(n1_tile, a, w)), held, ALU.add)
 
-        def z_view(a, w):
+        def z_values(a, w):
             return z_half[a // HALF][:, PACK * (a % HALF) : PACK * (a % HALF + w)]
-
-        def root(src, a, w, pair):
-            dst = z_view(a, w).rearrange("p (n t) -> p n t", t=PACK)[:, :, 2 * pair : 2 * pair + 2]
-            nc.scalar.activation(dst, src, ACT.Sqrt)
-
-        def root01(a, w):
-            root(sums01[:].rearrange("p (t n) -> p n t", t=2)[:, a : a + w, :], a, w, 0)
-
-        def root23(c):
-            root(sums23[c].rearrange("p (t n) -> p n t", t=2), chunks[c][0], chunks[c][1], 1)
-
-        def h_bank(t, a, w):
-            if t == 0 and a == HALF + QUARTER:
-                return y[2][:, 0:w]
-            if t == 0 and a >= HALF:
-                return y[t][:, a - HALF : a - HALF + w]
-            return h[t][:, a : a + w]
 
         def z_planes(a, w):
             cols = slice(a % HALF, a % HALF + w)
             return z_codes[a // HALF][:, cols].bitcast(FP8X4), z_scales[a // HALF][:, cols]
 
-        def quantise(c):
-            nc.vector.quantize_mx(*z_planes(*chunks[c]), z_view(*chunks[c]))
+        def root(a, w):
+            src = sum_rows(a, w).rearrange("p t (n i) -> p n t i", i=RUN)
+            nc.scalar.activation(z_values(a, w).rearrange("p (n i t) -> p n t i", i=RUN, t=PACK), src, ACT.Sqrt)
+
+        def quantise_z(a, w):
+            nc.vector.quantize_mx(*z_planes(a, w), z_values(a, w))
+
+        def deal_w2(pair):
+            src = w2_signed[:].rearrange("p j (m t) -> p t m j", t=PACK)[:, 2 * pair : 2 * pair + 2]
+            nc.scalar.copy(w2_dealt[pair][:].rearrange("p (t m j) -> p t m j", t=2, j=PACK), src)
+
+        def quantise_w2(pair):
+            cols = slice(HALF * pair, HALF * (pair + 1))
+            nc.vector.quantize_mx(w2_codes[:, cols].bitcast(FP8X4), w2_scales[:, cols], w2_dealt[pair][:])
+
+        def h_piece(t, a, w):
+            if t == 0:
+                return bank[{EARLY: 5, MIDDLE: 0, LAST: 2}[(a, w)]][:, 0:w]
+            return bank[{1: 6, 2: 7, 3: 1}[t]][:, a : a + w]
 
         def second_product(t, a, w):
             cols = slice(P * t, P * (t + 1))
-            nc.tensor.matmul_mx(h_bank(t, a, w), w2_codes[:, cols].bitcast(FP8X4), w2_scales[:, cols], *z_planes(a, w), start=True, stop=True)
+            nc.tensor.matmul_mx(h_piece(t, a, w), w2_codes[:, cols].bitcast(FP8X4), w2_scales[:, cols], *z_planes(a, w), start=True, stop=True)
 
-        for t in range(2):
-            units = [(t, a, HALF, part[t][:, a : a + HALF], sums01[:, S * t + a : S * t + a + HALF]) for a in (0, HALF)]
-            first_neighbours(units)
-            second_neighbours(units)
-        for j in range(2, PACK):
-            nc.scalar.activation(w2_signed[:, j, HALF:N], w2_raw[1][:, j, :], ACT.Copy, scale=g_sign[:, j : j + 1])
-        root01(0, HALF)
-        root01(HALF, HALF)
+        for t in (0, 1):
+            for add in (add_n2, add_n1):
+                for a in (0, HALF):
+                    add(t, a, HALF, partial[t][:, a : a + HALF])
         deal_w2(0)
 
-        early = [(2, 0, HALF, part[0][:, 0:HALF], sums23[0][:, 0:HALF]), (3, 0, HALF, part[2][:, QUARTER : QUARTER + HALF], sums23[0][:, HALF:S])]
-        first_neighbours(early)
-        second_neighbours(early)
-        root23(0)
+        held_early = {2: partial[0][:, 0:HALF], 3: partial[2][:, QUARTER : QUARTER + HALF]}
+        held_late = {2: partial[2][:, 0:HALF], 3: partial[2][:, HALF:S]}
+        for add in (add_n2, add_n1):
+            for t in (2, 3):
+                add(t, *EARLY, held_early[t])
+        root(*EARLY)
         deal_w2(1)
-        late = [(t, HALF, HALF, part[2][:, HALF * (t - 2) : HALF * (t - 1)], None) for t in (2, 3)]
-        first_neighbours(late)
+        for t in (2, 3):
+            add_n2(t, HALF, HALF, held_late[t])
         quantise_w2(0)
-        quantise(0)
-        second_product(0, 0, HALF)
-        second_product(1, 0, HALF)
-        for c in (1, 2):
-            a, w = chunks[c]
-            second_neighbours([(t, a, w, tmp[:, a - HALF : a - HALF + w], sums23[c][:, w * (t - 2) : w * (t - 1)]) for t, a0, w0, tmp, total in late])
-            if c == 1:
-                nc.scalar.copy(window[0][:, 0:HALF], h[0][:, 0:HALF])
-                nc.scalar.copy(plain[0][:, 0:HALF], h[0][:, 0:HALF])
-            root23(c)
-        quantise(1)
-        second_product(0, *chunks[1])
-        nc.scalar.activation(gate[0][:, 0:LEAD], plain[0][:, 0:LEAD], ACT.Sigmoid)
-        quantise(2)
-        second_product(0, *chunks[2])
-        for a, w in chunks[1:]:
-            nc.vector.tensor_copy(window[0][:, a : a + w], h_bank(0, a, w))
-            nc.vector.tensor_copy(plain[0][:, a : a + w], h_bank(0, a, w))
+        quantise_z(*EARLY)
+        for t in (0, 1):
+            second_product(t, *EARLY)
+        nc.scalar.copy(h_window[0][:, 0:HALF], h_piece(0, *EARLY))
+        for a, w in (MIDDLE, LAST):
+            for t in (2, 3):
+                add_n1(t, a, w, held_late[t][:, a - HALF : a - HALF + w])
+            root(a, w)
+
+        quantise_z(*MIDDLE)
+        second_product(0, *MIDDLE)
+        nc.scalar.activation(gate[0][:, 0:LEAD], h_window[0][:, 0:LEAD], ACT.Sigmoid)
+        nc.vector.tensor_copy(h_plain[0][:, 0:HALF], h_piece(0, *EARLY))
+        quantise_z(*LAST)
+        second_product(0, *LAST)
+        for a, w in (MIDDLE, LAST):
+            nc.vector.tensor_copy(h_window[0][:, a : a + w], h_piece(0, a, w))
+            nc.vector.tensor_copy(h_plain[0][:, a : a + w], h_piece(0, a, w))
         quantise_w2(1)
-        nc.vector.tensor_copy(window[1][:, 0:HALF], h[1][:, 0:HALF])
+        nc.vector.tensor_copy(h_window[1][:, 0:HALF], h_piece(1, *EARLY))
         second_product(1, HALF, HALF)
         for t in (2, 3):
             for a in (0, HALF):
@@ -249,30 +228,34 @@ def tile_picked_quadmean_none_p_kernel(tc, x_words, x_scales, w1, gn, w2, offs, 
 
         out_rows = out.rearrange("(p t) n -> p t n", t=PACK)
 
-        def gather(t, a, w):
-            nc.vector.tensor_tensor(diff[t][:, a : a + w], window[t][:].indirect(entries(n3_t, a, w)), plain[t][:, a : a + w], ALU.subtract)
+        def copy_h(t, a):
+            nc.scalar.copy(h_window[t][:, a:S], h_piece(t, a, S - a))
+            nc.scalar.copy(h_plain[t][:], h_piece(t, 0, S))
+
+        def subtract_n3(t, a, w):
+            nc.vector.tensor_tensor(diff[t][:, a : a + w], h_window[t][:].indirect(entries(n3_tile, a, w)), h_plain[t][:, a : a + w], ALU.subtract)
+
+        def sigmoid(t, a):
+            nc.scalar.activation(gate[t][:, a:S], h_plain[t][:, a:S], ACT.Sigmoid)
 
         def finish(t, a, w):
-            nc.vector.scalar_tensor_tensor(res[t][:, a : a + w], diff[t][:, a : a + w], -1.0, gate[t][:, a : a + w], ALU.mult, ALU.mult)
-            nc.sync.dma_start(out_rows[:, t, a : a + w], res[t][:, a : a + w])
+            nc.vector.scalar_tensor_tensor(result[t][:, a : a + w], diff[t][:, a : a + w], -1.0, gate[t][:, a : a + w], ALU.mult, ALU.mult)
+            nc.sync.dma_start(out_rows[:, t, a : a + w], result[t][:, a : a + w])
 
-        gather(0, 0, HALF)
-        gather(0, HALF, HALF)
-        for t in range(1, PACK):
-            a = HALF if t == 1 else 0
-            if t == 3:
-                nc.scalar.activation(gate[2][:], plain[2][:], ACT.Sigmoid)
-                finish(2, 0, S)
-            nc.scalar.copy(window[t][:, a:S], h_bank(t, a, S - a))
-            nc.scalar.copy(plain[t][:], h_bank(t, 0, S))
-            if t == 3:
-                break
-            gather(t, 0, S)
-            a = LEAD if t == 1 else 0
-            nc.scalar.activation(gate[t - 1][:, a:S], plain[t - 1][:, a:S], ACT.Sigmoid)
-            finish(t - 1, 0, S)
-        gather(3, 0, HALF)
-        gather(3, HALF, HALF)
-        nc.scalar.activation(gate[3][:], plain[3][:], ACT.Sigmoid)
-        finish(3, 0, HALF)
-        finish(3, HALF, HALF)
+        for a in (0, HALF):
+            subtract_n3(0, a, HALF)
+        copy_h(1, HALF)
+        subtract_n3(1, 0, S)
+        sigmoid(0, LEAD)
+        finish(0, 0, S)
+        copy_h(2, 0)
+        subtract_n3(2, 0, S)
+        for t in (1, 2):
+            sigmoid(t, 0)
+            finish(t, 0, S)
+        copy_h(3, 0)
+        for a in (0, HALF):
+            subtract_n3(3, a, HALF)
+        sigmoid(3, 0)
+        for a in (0, HALF):
+            finish(3, a, HALF)

@@ -22,7 +22,6 @@ LIST_ROWS = 16
 HALF = 256
 QUARTER = 128
 GROUPS = HALF // PACK
-RUN = 4
 W1_ON_VECTOR = 36
 LEAD = 32
 
@@ -51,14 +50,20 @@ def tile_picked_quadmean_none_p_kernel(tc, x_words, x_scales, w1, gn, w2, offs, 
         nc.gpsimd.memset(table_scales[:].bitcast(I32), 0)
         nc.scalar.dma_start(gain[:], gn.rearrange("(p t) o -> p (t o)", t=PACK))
         nc.sync.dma_start(offs_tile[:], offs)
-        nc.sync.dma_start(table_words[:], x_words[0].rearrange("p n j -> p (n j)").bitcast(I32))
+
+        def load_half(raw, weight, c):
+            nc.sync.dma_start(raw[c][:], weight.rearrange("(p j) n -> p j n", j=PACK)[:, :, HALF * c : HALF * (c + 1)])
+
+        load_half(w1_raw, w1, 0)
         for q in range(4):
             nc.sync.dma_start(table_scales[32 * q : 32 * q + 4, :].bitcast(I32), x_scales[0, 4 * q : 4 * q + 4, :].bitcast(I32))
-        for raw, weight in ((w1_raw, w1), (w2_raw, w2)):
-            for c in range(2):
-                nc.sync.dma_start(raw[c][:], weight.rearrange("(p j) n -> p j n", j=PACK)[:, :, HALF * c : HALF * (c + 1)])
-        for list_tile, source in ((n2_tile, n2), (n1_tile, n1), (n3_tile, n3)):
-            nc.sync.dma_start(list_tile[:], source)
+        load_half(w1_raw, w1, 1)
+        nc.sync.dma_start(table_words[:], x_words[0].rearrange("p n j -> p (n j)").bitcast(I32))
+        load_half(w2_raw, w2, 0)
+        nc.sync.dma_start(n2_tile[:], n2)
+        nc.sync.dma_start(n1_tile[:], n1)
+        load_half(w2_raw, w2, 1)
+        nc.sync.dma_start(n3_tile[:], n3)
 
         one_quarter = sb("one_quarter", [P, 1], F32)
         one_half = sb("one_half", [P, 1], F32)
@@ -73,8 +78,9 @@ def tile_picked_quadmean_none_p_kernel(tc, x_words, x_scales, w1, gn, w2, offs, 
 
         x_codes = sb("x_codes", [P, S], U32)
         x_bytes = sb("x_bytes", [P, S], U8)
-        nc.vector.tensor_copy(x_codes[:], table_words[:].bitcast(U32).indirect(offs_tile[:]))
         nc.vector.tensor_copy(x_bytes[:], table_scales[:].indirect(offs_tile[:]))
+        for a in (0, HALF):
+            nc.vector.tensor_copy(x_codes[:, a : a + HALF], table_words[:].bitcast(U32).indirect(entries(offs_tile, a, HALF)))
 
         w1_dealt = sb("w1_dealt", [P, PACK * H], BF16)
         w1_codes = sb("w1_codes", [P, H], U32)
@@ -99,7 +105,8 @@ def tile_picked_quadmean_none_p_kernel(tc, x_words, x_scales, w1, gn, w2, offs, 
         term_n2 = [sb(f"term_n2_{t}", [P, S], F32) for t in range(PACK)]
         term_n1 = [sb(f"term_n1_{t}", [P, S], F32) for t in range(PACK)]
         term_own = [sb(f"term_own{t}", [P, S], F32) for t in range(PACK)]
-        w2_signed = sb("w2_signed", [P, PACK, N], BF16)
+        w2_dealt = sb("w2_dealt", [P, PACK * N], BF16)
+        w2_signed = sb("w2_signed", [P, PACK, HALF], BF16)
 
         def square(term, t, scale):
             for piece, a, b in y_pieces[t]:
@@ -108,8 +115,12 @@ def tile_picked_quadmean_none_p_kernel(tc, x_words, x_scales, w1, gn, w2, offs, 
         def own(t):
             nc.scalar.activation(term_own[t][:], term_n2[t][:], ACT.Identity, scale=4.0, bias=bias_own[:, t : t + 1])
 
-        for j in range(PACK):
-            nc.vector.tensor_scalar(w2_signed[:, j, 0:HALF], w2_raw[0][:, j, :], sign[:, j : j + 1], None, ALU.mult)
+        nc.vector.tensor_tensor(
+            w2_dealt[:].rearrange("p (t m j) -> p m j t", t=PACK, j=PACK)[:, 0:GROUPS],
+            w2_raw[0][:].rearrange("p j (m t) -> p m j t", t=PACK),
+            sign[:].unsqueeze(1).unsqueeze(3).to_broadcast([P, GROUPS, PACK, PACK]),
+            ALU.mult,
+        )
         square(term_n2, 0, scale_n2)
         for a in (0, HALF):
             nc.vector.tensor_scalar(term_own[0][:, a : a + HALF], term_n2[0][:, a : a + HALF], 4.0, bias_own[:, 0:1], ALU.mult, ALU.add)
@@ -122,7 +133,8 @@ def tile_picked_quadmean_none_p_kernel(tc, x_words, x_scales, w1, gn, w2, offs, 
         for t in (2, 3):
             own(t)
         for j in range(PACK):
-            nc.scalar.activation(w2_signed[:, j, HALF:N], w2_raw[1][:, j, :], ACT.Copy, scale=sign[:, j : j + 1])
+            dst = w2_signed[:, j, :].rearrange("p (t m) -> p m t", t=PACK)
+            nc.scalar.activation(dst, w2_raw[1][:, j, :].rearrange("p (m t) -> p m t", t=PACK), ACT.Copy, scale=sign[:, j : j + 1])
         for t in (2, 3):
             square(term_n1, t, scale_n1)
 
@@ -139,7 +151,6 @@ def tile_picked_quadmean_none_p_kernel(tc, x_words, x_scales, w1, gn, w2, offs, 
         z_half = [sb(f"z_half{c}", [P, PACK * HALF], BF16) for c in range(2)]
         z_codes = [sb(f"z_codes{c}", [P, HALF], U32) for c in range(2)]
         z_scales = [sb(f"z_scales{c}", [P, HALF], U8) for c in range(2)]
-        w2_dealt = [sb(f"w2_dealt{pair}", [P, 2 * N], BF16) for pair in range(2)]
         w2_codes = sb("w2_codes", [P, N], U32)
         w2_scales = sb("w2_scales", [P, N], U8)
 
@@ -162,19 +173,19 @@ def tile_picked_quadmean_none_p_kernel(tc, x_words, x_scales, w1, gn, w2, offs, 
             return z_codes[a // HALF][:, cols].bitcast(FP8X4), z_scales[a // HALF][:, cols]
 
         def root(a, w):
-            src = sum_rows(a, w).rearrange("p t (n i) -> p n t i", i=RUN)
-            nc.scalar.activation(z_values(a, w).rearrange("p (n i t) -> p n t i", i=RUN, t=PACK), src, ACT.Sqrt)
+            nc.scalar.activation(z_values(a, w).rearrange("p (n t) -> p n t", t=PACK), sum_rows(a, w).rearrange("p t n -> p n t"), ACT.Sqrt)
 
         def quantise_z(a, w):
             nc.vector.quantize_mx(*z_planes(a, w), z_values(a, w))
 
         def deal_w2(pair):
-            src = w2_signed[:].rearrange("p j (m t) -> p t m j", t=PACK)[:, 2 * pair : 2 * pair + 2]
-            nc.scalar.copy(w2_dealt[pair][:].rearrange("p (t m j) -> p t m j", t=2, j=PACK), src)
+            tiles = slice(2 * pair, 2 * pair + 2)
+            dst = w2_dealt[:].rearrange("p (t m j) -> p t m j", t=PACK, j=PACK)[:, tiles, GROUPS : 2 * GROUPS]
+            nc.scalar.copy(dst, w2_signed[:].rearrange("p j (t m) -> p t m j", t=PACK)[:, tiles])
 
         def quantise_w2(pair):
             cols = slice(HALF * pair, HALF * (pair + 1))
-            nc.vector.quantize_mx(w2_codes[:, cols].bitcast(FP8X4), w2_scales[:, cols], w2_dealt[pair][:])
+            nc.vector.quantize_mx(w2_codes[:, cols].bitcast(FP8X4), w2_scales[:, cols], w2_dealt[:, 2 * N * pair : 2 * N * (pair + 1)])
 
         def h_piece(t, a, w):
             if t == 0:
@@ -197,10 +208,10 @@ def tile_picked_quadmean_none_p_kernel(tc, x_words, x_scales, w1, gn, w2, offs, 
             for t in (2, 3):
                 add(t, *EARLY, held_early[t])
         root(*EARLY)
-        deal_w2(1)
         for t in (2, 3):
             add_n2(t, HALF, HALF, held_late[t])
         quantise_w2(0)
+        deal_w2(1)
         quantise_z(*EARLY)
         for t in (0, 1):
             second_product(t, *EARLY)

import math
from contextlib import ExitStack

import concourse.mybir as mybir

K, T, S, H, N = 512, 2048, 512, 512, 512
FLOPS = 2 * K * H * S + 2 * H * N * S

F32 = mybir.dt.float32
BF16 = mybir.dt.bfloat16
I32 = mybir.dt.int32
U32 = mybir.dt.uint32
U16 = mybir.dt.uint16
U8 = mybir.dt.uint8
FP8X4 = mybir.dt.float8_e4m3fn_x4
ACT = mybir.ActivationFunctionType
ALU = mybir.AluOpType

P = 128
PACK = 4
LIST_ROWS = 16
HALF = 256
QUARTER = 128
GROUPS = HALF // PACK
W1_ON_VECTOR = 36
LEAD = 32

EARLY, MIDDLE, LAST = (0, HALF), (HALF + QUARTER, QUARTER), (HALF, QUARTER)


def tile_picked_quadmean_none_p_kernel(tc, x_words, x_scales, w1, gn, w2, offs, n1, n2, n3, out):
    nc = tc.nc
    with ExitStack() as ctx:
        keep = ctx.enter_context(tc.tile_pool(name="keep", bufs=1))
        psum = ctx.enter_context(tc.psum_pool(name="psum", bufs=1))

        def sb(name, shape, dtype):
            return keep.tile(shape, dtype, name=name, align_bytes=64)

        def entries(list_tile, a, w):
            return list_tile[:, a // LIST_ROWS : (a + w) // LIST_ROWS]

        offs_tile, n1_tile, n2_tile, n3_tile = [sb(name, [P, S // LIST_ROWS], U16) for name in ("offs_tile", "n1_tile", "n2_tile", "n3_tile")]
        table_words = sb("table_words", [P, T], I32)
        table_scales = sb("table_scales", [P, T], U8)
        gain = sb("gain", [P, PACK], F32)
        w1_raw = [sb(f"w1_raw{c}", [P, PACK, HALF], F32) for c in range(2)]
        w2_raw = [sb(f"w2_raw{c}", [P, PACK, HALF], F32) for c in range(2)]

        nc.gpsimd.memset(table_scales[:].bitcast(I32), 0)
        nc.scalar.dma_start(gain[:], gn.rearrange("(p t) o -> p (t o)", t=PACK))
        nc.sync.dma_start(offs_tile[:], offs)

        def load_half(raw, weight, c):
            nc.sync.dma_start(raw[c][:], weight.rearrange("(p j) n -> p j n", j=PACK)[:, :, HALF * c : HALF * (c + 1)])

        load_half(w1_raw, w1, 0)
        for q in range(4):
            nc.sync.dma_start(table_scales[32 * q : 32 * q + 4, :].bitcast(I32), x_scales[0, 4 * q : 4 * q + 4, :].bitcast(I32))
        load_half(w1_raw, w1, 1)
        nc.sync.dma_start(table_words[:], x_words[0].rearrange("p n j -> p (n j)").bitcast(I32))
        load_half(w2_raw, w2, 0)
        nc.sync.dma_start(n2_tile[:], n2)
        nc.sync.dma_start(n1_tile[:], n1)
        load_half(w2_raw, w2, 1)
        nc.sync.dma_start(n3_tile[:], n3)

        one_quarter = sb("one_quarter", [P, 1], F32)
        one_half = sb("one_half", [P, 1], F32)
        nc.gpsimd.memset(one_quarter[:], 0.25)
        nc.scalar.activation(one_half[:], one_quarter[:], ACT.Sqrt)
        scale_n2, scale_n1, bias_own, sign_or_zero, sign = [sb(name, [P, PACK], F32) for name in ("scale_n2", "scale_n1", "bias_own", "sign_or_zero", "sign")]
        nc.scalar.activation(sign_or_zero[:], gain[:], ACT.Sign)
        nc.scalar.activation(scale_n2[:], gain[:], ACT.Copy, scale=0.5)
        nc.scalar.activation(scale_n1[:], gain[:], ACT.Copy, scale=math.sqrt(0.5))
        nc.scalar.activation(bias_own[:], gain[:], ACT.Square, scale=math.sqrt(0.1))
        nc.scalar.activation(sign[:], sign_or_zero[:], ACT.Sign, bias=one_half[:])

        x_codes = sb("x_codes", [P, S], U32)
        x_bytes = sb("x_bytes", [P, S], U8)
        nc.vector.tensor_copy(x_bytes[:], table_scales[:].indirect(offs_tile[:]))
        for a in (0, HALF):
            nc.vector.tensor_copy(x_codes[:, a : a + HALF], table_words[:].bitcast(U32).indirect(entries(offs_tile, a, HALF)))

        w1_dealt = sb("w1_dealt", [P, PACK * H], BF16)
        w1_codes = sb("w1_codes", [P, H], U32)
        w1_scales = sb("w1_scales", [P, H], U8)

        def deal_w1(copy, c, m0, m1):
            dst = w1_dealt[:].rearrange("p (t m j) -> p m j t", t=PACK, j=PACK)[:, GROUPS * c + m0 : GROUPS * c + m1]
            copy(dst, w1_raw[c][:].rearrange("p j (m t) -> p m j t", t=PACK)[:, m0:m1])

        deal_w1(nc.scalar.copy, 0, 0, GROUPS)
        deal_w1(nc.vector.tensor_copy, 1, 0, W1_ON_VECTOR)
        deal_w1(nc.scalar.copy, 1, W1_ON_VECTOR, GROUPS)

        bank = [psum.tile([P, S], F32, name=f"bank{b}") for b in range(8)]
        y_pieces = [[(bank[0][:, 0:HALF], 0, HALF), (bank[4][:, 0:HALF], HALF, S)]] + [[(bank[t][:], 0, S)] for t in range(1, PACK)]
        for t in range(PACK):
            cols = slice(P * t, P * (t + 1))
            nc.vector.quantize_mx(w1_codes[:, cols].bitcast(FP8X4), w1_scales[:, cols], w1_dealt[:, PACK * P * t : PACK * P * (t + 1)])
            for piece, a, b in y_pieces[t]:
                nc.tensor.matmul_mx(piece, w1_codes[:, cols].bitcast(FP8X4), w1_scales[:, cols], x_codes[:, a:b].bitcast(FP8X4), x_bytes[:, a:b], start=True, stop=True)

        term_n2 = [sb(f"term_n2_{t}", [P, S], F32) for t in range(PACK)]
        term_n1 = [sb(f"term_n1_{t}", [P, S], F32) for t in range(PACK)]
        term_own = [sb(f"term_own{t}", [P, S], F32) for t in range(PACK)]
        w2_dealt = sb("w2_dealt", [P, PACK * N], BF16)
        w2_signed = sb("w2_signed", [P, PACK, HALF], BF16)

        def square(term, t, scale):
            for piece, a, b in y_pieces[t]:
                nc.scalar.activation(term[t][:, a:b], piece, ACT.Square, scale=scale[:, t : t + 1])

        def own(t):
            nc.scalar.activation(term_own[t][:], term_n2[t][:], ACT.Identity, scale=4.0, bias=bias_own[:, t : t + 1])

        nc.vector.tensor_tensor(
            w2_dealt[:].rearrange("p (t m j) -> p m j t", t=PACK, j=PACK)[:, 0:GROUPS],
            w2_raw[0][:].rearrange("p j (m t) -> p m j t", t=PACK),
            sign[:].unsqueeze(1).unsqueeze(3).to_broadcast([P, GROUPS, PACK, PACK]),
            ALU.mult,
        )
        square(term_n2, 0, scale_n2)
        for a in (0, HALF):
            nc.vector.tensor_scalar(term_own[0][:, a : a + HALF], term_n2[0][:, a : a + HALF], 4.0, bias_own[:, 0:1], ALU.mult, ALU.add)
        square(term_n1, 0, scale_n1)
        square(term_n2, 1, scale_n2)
        square(term_n1, 1, scale_n1)
        own(1)
        for t in (2, 3):
            square(term_n2, t, scale_n2)
        for t in (2, 3):
            own(t)
        for j in range(PACK):
            dst = w2_signed[:, j, :].rearrange("p (t m) -> p m t", t=PACK)
            nc.scalar.activation(dst, w2_raw[1][:, j, :].rearrange("p (m t) -> p m t", t=PACK), ACT.Copy, scale=sign[:, j : j + 1])
        for t in (2, 3):
            square(term_n1, t, scale_n1)

        h_window = [sb(f"h_window{t}", [P, 2 * S if t in (1, 2) else S], F32) for t in range(PACK)]
        for t in (1, 2):
            nc.gpsimd.memset(h_window[t][:, S : 2 * S], 0.0)
        h_plain = [sb(f"h_plain{t}", [P, S], F32) for t in range(PACK)]

        sums = sb("sums", [P, 6 * HALF], F32)
        gate = [sums[:, 2 * HALF : 4 * HALF]] + [sb(f"gate{t}", [P, S], F32)[:] for t in range(1, PACK)]
        partial = [sb(f"partial{i}", [P, S], F32) for i in range(3)]
        diff = [sb(f"diff{t}", [P, S], F32) for t in range(PACK)]
        result = [sb(f"result{t}", [P, S], F32) for t in range(PACK)]
        z_half = [sb(f"z_half{c}", [P, PACK * HALF], BF16) for c in range(2)]
        z_codes = [sb(f"z_codes{c}", [P, HALF], U32) for c in range(2)]
        z_scales = [sb(f"z_scales{c}", [P, HALF], U8) for c in range(2)]
        w2_codes = sb("w2_codes", [P, N], U32)
        w2_scales = sb("w2_scales", [P, N], U8)

        def sum_rows(a, w):
            first_row = 2 if a < HALF else 0
            rows = sums[:, first_row * HALF : (first_row + PACK) * HALF].rearrange("p (t n) -> p t n", t=PACK)
            return rows[:, :, a % HALF : a % HALF + w]

        def add_n2(t, a, w, held):
            nc.vector.tensor_tensor(held, term_n2[t][:].indirect(entries(n2_tile, a, w)), term_own[t][:, a : a + w], ALU.add)

        def add_n1(t, a, w, held):
            nc.vector.tensor_tensor(sum_rows(a, w)[:, t], term_n1[t][:].indirect(entries(n1_tile, a, w)), held, ALU.add)

        def z_values(a, w):
            return z_half[a // HALF][:, PACK * (a % HALF) : PACK * (a % HALF + w)]

        def z_planes(a, w):
            cols = slice(a % HALF, a % HALF + w)
            return z_codes[a // HALF][:, cols].bitcast(FP8X4), z_scales[a // HALF][:, cols]

        def root(a, w):
            nc.scalar.activation(z_values(a, w).rearrange("p (n t) -> p n t", t=PACK), sum_rows(a, w).rearrange("p t n -> p n t"), ACT.Sqrt)

        def quantise_z(a, w):
            nc.vector.quantize_mx(*z_planes(a, w), z_values(a, w))

        def deal_w2(pair):
            tiles = slice(2 * pair, 2 * pair + 2)
            dst = w2_dealt[:].rearrange("p (t m j) -> p t m j", t=PACK, j=PACK)[:, tiles, GROUPS : 2 * GROUPS]
            nc.scalar.copy(dst, w2_signed[:].rearrange("p j (t m) -> p t m j", t=PACK)[:, tiles])

        def quantise_w2(pair):
            cols = slice(HALF * pair, HALF * (pair + 1))
            nc.vector.quantize_mx(w2_codes[:, cols].bitcast(FP8X4), w2_scales[:, cols], w2_dealt[:, 2 * N * pair : 2 * N * (pair + 1)])

        def h_piece(t, a, w):
            if t == 0:
                return bank[{EARLY: 5, MIDDLE: 0, LAST: 2}[(a, w)]][:, 0:w]
            return bank[{1: 6, 2: 7, 3: 1}[t]][:, a : a + w]

        def second_product(t, a, w):
            cols = slice(P * t, P * (t + 1))
            nc.tensor.matmul_mx(h_piece(t, a, w), w2_codes[:, cols].bitcast(FP8X4), w2_scales[:, cols], *z_planes(a, w), start=True, stop=True)

        for t in (0, 1):
            for add in (add_n2, add_n1):
                for a in (0, HALF):
                    add(t, a, HALF, partial[t][:, a : a + HALF])
        deal_w2(0)

        held_early = {2: partial[0][:, 0:HALF], 3: partial[2][:, QUARTER : QUARTER + HALF]}
        held_late = {2: partial[2][:, 0:HALF], 3: partial[2][:, HALF:S]}
        for add in (add_n2, add_n1):
            for t in (2, 3):
                add(t, *EARLY, held_early[t])
        root(*EARLY)
        for t in (2, 3):
            add_n2(t, HALF, HALF, held_late[t])
        quantise_w2(0)
        deal_w2(1)
        quantise_z(*EARLY)
        for t in (0, 1):
            second_product(t, *EARLY)
        nc.scalar.copy(h_window[0][:, 0:HALF], h_piece(0, *EARLY))
        for a, w in (MIDDLE, LAST):
            for t in (2, 3):
                add_n1(t, a, w, held_late[t][:, a - HALF : a - HALF + w])
            root(a, w)

        quantise_z(*MIDDLE)
        second_product(0, *MIDDLE)
        nc.scalar.activation(gate[0][:, 0:LEAD], h_window[0][:, 0:LEAD], ACT.Sigmoid)
        nc.vector.tensor_copy(h_plain[0][:, 0:HALF], h_piece(0, *EARLY))
        quantise_z(*LAST)
        second_product(0, *LAST)
        for a, w in (MIDDLE, LAST):
            nc.vector.tensor_copy(h_window[0][:, a : a + w], h_piece(0, a, w))
            nc.vector.tensor_copy(h_plain[0][:, a : a + w], h_piece(0, a, w))
        quantise_w2(1)
        nc.vector.tensor_copy(h_window[1][:, 0:HALF], h_piece(1, *EARLY))
        second_product(1, HALF, HALF)
        for t in (2, 3):
            for a in (0, HALF):
                second_product(t, a, HALF)

        out_rows = out.rearrange("(p t) n -> p t n", t=PACK)

        def copy_h(t, a):
            nc.scalar.copy(h_window[t][:, a:S], h_piece(t, a, S - a))
            nc.scalar.copy(h_plain[t][:], h_piece(t, 0, S))

        def subtract_n3(t, a, w):
            nc.vector.tensor_tensor(diff[t][:, a : a + w], h_window[t][:].indirect(entries(n3_tile, a, w)), h_plain[t][:, a : a + w], ALU.subtract)

        def sigmoid(t, a):
            nc.scalar.activation(gate[t][:, a:S], h_plain[t][:, a:S], ACT.Sigmoid)

        def finish(t, a, w):
            nc.vector.scalar_tensor_tensor(result[t][:, a : a + w], diff[t][:, a : a + w], -1.0, gate[t][:, a : a + w], ALU.mult, ALU.mult)
            nc.sync.dma_start(out_rows[:, t, a : a + w], result[t][:, a : a + w])

        for a in (0, HALF):
            subtract_n3(0, a, HALF)
        copy_h(1, HALF)
        subtract_n3(1, 0, S)
        sigmoid(0, LEAD)
        finish(0, 0, S)
        copy_h(2, 0)
        subtract_n3(2, 0, S)
        for t in (1, 2):
            sigmoid(t, 0)
            finish(t, 0, S)
        copy_h(3, 0)
        for a in (0, HALF):
            subtract_n3(3, a, HALF)
        sigmoid(3, 0)
        for a in (0, HALF):
            finish(3, a, HALF)
